import numpy as np, ml_dtypes
CORES = [19,147,275,403]
N = 4
import mx_ref
NC, G = 128, 2
C = np.float32(0.019)
BF = ml_dtypes.bfloat16
def cut(t, i, w=512):
    return t[:, w * i:w * i + w]
def tile(rs):
    return np.stack(rs, axis=2).reshape(128, -1).astype(BF)
def layer(w, X):
    out = []
    for i in range(G):
        for t in range(len(X)):
            p = mx_ref.matmul(mx_ref.quantize(cut(w, len(X) * i + t)), X[t])
            z = p if t == 0 else z + p
        out.append(z)
    return out
def act(Z):
    return [np.maximum(s * z, 0) * C for z in Z for s in (1, -1)]
def pick(b):
    s = np.zeros((128, 128, 4), np.float32)
    s[np.arange(128), np.arange(128), b] = 1.0
    return mx_ref.quantize(s.reshape(128, 512).astype(BF))
def setup_inputs(rng):
    def f(*shape):
        return mx_ref.flush((rng.standard_normal(shape, dtype=np.float32) * np.exp2(rng.integers(-2, 3, shape[:-1] + (1,)))).astype(BF))
    return {"a": f(N, 128, G * 512), "b": f(N, 128, N * 4 * NC)}
def setup_inputs_blocks(rng):
    d = setup_inputs(rng)
    for k in ("a", "b"): d[k] = mx_ref.spread(d[k], rng, 4)
    return d
def setup_inputs_wide(rng):
    d = setup_inputs(rng)
    for k in ("a", "b"): d[k] = mx_ref.flush((d[k].astype(np.float32) * np.exp2(rng.integers(-8, 9, (N, 1, 1))).astype(np.float32)).astype(BF))
    return d
def reference(a, b):
    S = [pick(t) for t in range(4)]
    y = np.zeros((N, 128, NC, 4), np.float32)
    for c in range(N):
        for r in range(N):
            q = mx_ref.quantize(tile(act(layer(a[r], [mx_ref.quantize(cut(b[r], c, 4 * NC))]))))
            p = np.stack([mx_ref.matmul(S[t], q) for t in range(4)], axis=2)
            y[c] = p if r == 0 else y[c] + p
    return {"y": y.reshape(N, 128, 4 * NC)}

import numpy as np
from concourse.mybir import dt, AluOpType, ActivationFunctionType

N = 4
NW = 128
SIM_CORES = 512
C = float(np.float32(0.019))

SCRATCH = {
    "abuf": ("sbuf", [128, 1024], "bfloat16"),
    "bbuf": ("sbuf", [128, 2048], "bfloat16"),
    "aq": ("sbuf", [128, 256], "float8_e4m3fn_x4"),
    "asc": ("sbuf", [128, 256], "uint8"),
    "bq": ("sbuf", [128, 512], "float8_e4m3fn_x4"),
    "bsc": ("sbuf", [128, 512], "uint8"),
    "gt": ("sbuf", [128, 2048], "bfloat16"),
    "eye": ("sbuf", [128, 128], "bfloat16"),
    "et": ("sbuf", [128, 1024], "bfloat16"),
    "sq": ("sbuf", [128, 512], "float8_e4m3fn_x4"),
    "ssc": ("sbuf", [128, 512], "uint8"),
    "ybuf": ("sbuf", [128, 512], "float32"),
    "zp": ("psum", [128, 2048], "float32"),
    "dp": ("psum", [128, 2048], "float32"),
}
for _r in range(N):
    for _c in range(N):
        SCRATCH["g%d%dq" % (_r, _c)] = ("sbuf", [128, NW], "float8_e4m3fn_x4")
        SCRATCH["g%d%dsc" % (_r, _c)] = ("sbuf", [128, NW], "uint8")
SEMAPHORES = (["mI", "mE", "aI", "cE", "sQ", "lA", "qA0", "qA1", "yc", "st",
               "rc", "rs", "pa", "ca", "fa", "sx", "sh", "sent"]
              + ["%s%d" % (n, k) for n in ("lB", "qB", "z0", "z1", "av", "as", "gQ", "dF") for k in range(4)])

_PLAN = {}


def _plan(T, topo):
    if _PLAN:
        return _PLAN
    cores = list(T.cores)
    for x in cores:
        part = [c for c in cores if c != x and topo.rack(topo.host(c)) == topo.rack(topo.host(x))][0]
        far = [c for c in cores if c not in (x, part) and topo.may_write(x, c)][0]
        diag = [c for c in cores if c not in (x, part, far)][0]
        helper = [c for c in range(SIM_CORES)
                  if c not in cores and topo.host(c) == topo.host(x) and topo.chip(c) == topo.chip(x)
                  and topo.die(c) == topo.die(x) and topo.may_write(c, far) and topo.may_write(c, x)][0]
        _PLAN[x] = (part, far, diag, helper)
    return _PLAN


def _bits(mask):
    return bin(mask).count("1")


def _cols(k, n=1):
    return slice(NW * k, NW * (k + n))


def _send(g, T, topo, src, dst, buf, cols, rsem, mask):
    rid, pid = topo.addr(dst, src)
    ap = T[buf][:, cols]
    if buf.endswith("q"):
        ap = ap.bitcast(dt.uint8)
    g.remote_dma(out_ap=ap, in_ap=ap, remote_sem=T.sem[rsem], local_sem=T.sem.sent, pid=pid, routing_id=rid,
                 dma_engine_mask=mask)
    return _bits(mask)


def _make_picks(g, T, bs):
    s, v = T.sem, g.vector
    n = len(bs)
    v.memset(T.eye[:], 1.0).then_inc(s.mI, 1)
    v.memset(T.et[:, 0:512 * n], 0.0).then_inc(s.mE, 1)
    g.wait_ge(s.mI, 1)
    g.affine_select(T.eye[:], T.eye[:], [[-1, 128]], AluOpType.is_equal, 0.0, 0, 1).then_inc(s.aI, 1)
    v.wait_ge(s.aI, 1)
    v.wait_ge(s.mE, 1)
    for i, b in enumerate(bs):
        v.tensor_copy(T.et[:, 512 * i + b:512 * (i + 1):4], T.eye[:]).then_inc(s.cE, 1)
    v.wait_ge(s.cE, n)
    v.quantize_mx(T.sq[:, _cols(bs[0], n)], T.ssc[:, _cols(bs[0], n)], T.et[:, 0:512 * n]).then_inc(s.sQ, 1)


def _helper_program(g, core, T, topo, x, part, far):
    s = T.sem
    mask = topo.mask(core, far) & topo.mask(core, x)
    _make_picks(g, T, [2, 3])
    g.wait_ge(s.sQ, 1)
    left = _send(g, T, topo, core, x, "sq", _cols(2, 2), "sh", mask)
    left += _send(g, T, topo, core, x, "ssc", _cols(2, 2), "sh", mask)
    ne = _bits(topo.mask(part, core))
    name = "g%d%d" % (T.rank_of(part), T.rank_of(far))
    g.wait_ge(s.rc, ne)
    left += _send(g, T, topo, core, far, name + "q", _cols(0), "fa", mask)
    g.wait_ge(s.rs, ne)
    left += _send(g, T, topo, core, far, name + "sc", _cols(0), "fa", mask)
    g.wait_ge(s.sent, left)


def rank_program(g, core, T, topo):
    plan = _plan(T, topo)
    rank = T.rank_of(core)
    if rank is None:
        for x in plan:
            if plan[x][3] == core:
                _helper_program(g, core, T, topo, x, plan[x][0], plan[x][1])
        return
    part, far, diag, helper = plan[core]
    relay = plan[part][3]
    s, v, sc, te, sy = T.sem, g.vector, g.scalar, g.tensor, g.sync
    dest = [diag, part, far, core]
    own = ["g%d%d" % (rank, T.rank_of(d)) for d in dest]
    mine = 0 if core < part else 1

    def load_b(q, k):
        c = T.rank_of(dest[k])
        q.dma_start(T.bbuf[:, 512 * k:512 * (k + 1)], T.b[:, 512 * c:512 * (c + 1)]).then_inc(s["lB%d" % k], 16)
    sy.dma_start(T.abuf[:], T.a[:, :]).then_inc(s.lA, 16)
    load_b(sc, 0)
    load_b(sy, 1)
    load_b(sc, 2)
    load_b(sy, 3)

    _make_picks(g, T, [mine])
    m_part, m_far, m_relay = topo.mask(core, part), topo.mask(core, far), topo.mask(core, relay)
    g.wait_ge(s.sQ, 1)
    left = _send(g, T, topo, core, part, "sq", _cols(mine), "sx", m_part)
    left += _send(g, T, topo, core, part, "ssc", _cols(mine), "sx", m_part)

    def quant_b(k):
        v.wait_ge(s["lB%d" % k], 16)
        v.quantize_mx(T.bq[:, _cols(k)], T.bsc[:, _cols(k)], T.bbuf[:, 512 * k:512 * (k + 1)]).then_inc(s["qB%d" % k], 1)

    def bank(k, i):
        j = 2 * (k % 2) + i
        return T.zp[:, 512 * j:512 * j + NW]

    def act_v(k):
        v.wait_ge(s["z0%d" % k], 1)
        for b, c in ((0, C), (1, -C)):
            v.tensor_scalar(T.gt[:, 512 * k + b:512 * (k + 1):4], bank(k, 0), c, 0.0,
                            AluOpType.mult, AluOpType.max).then_inc(s["av%d" % k], 1)

    def quant_g(k):
        v.wait_ge(s["av%d" % k], 2)
        v.wait_ge(s["as%d" % k], 2)
        v.quantize_mx(T[own[k] + "q"][:], T[own[k] + "sc"][:], T.gt[:, 512 * k:512 * (k + 1)]).then_inc(s["gQ%d" % k], 1)

    quant_b(0)
    v.wait_ge(s.lA, 16)
    for i in range(2):
        v.quantize_mx(T.aq[:, _cols(i)], T.asc[:, _cols(i)], T.abuf[:, 512 * i:512 * (i + 1)]).then_inc(s["qA%d" % i], 1)
    act_v(0)
    quant_g(0)
    quant_b(1)
    act_v(1)
    quant_b(2)
    quant_g(1)
    act_v(2)
    quant_b(3)
    quant_g(2)
    act_v(3)
    quant_g(3)

    for k in range(4):
        sc.wait_ge(s["z1%d" % k], 1)
        for b, c in ((2, C), (3, -C)):
            sc.activation(T.gt[:, 512 * k + b:512 * (k + 1):4], bank(k, 1), ActivationFunctionType.Relu,
                          scale=c).then_inc(s["as%d" % k], 1)

    for k in range(4):
        te.wait_ge(s["qB%d" % k], 1)
        if k >= 2:
            te.wait_ge(s["gQ%d" % (k - 2)], 1)
        for i in range(2):
            if k == 0:
                te.wait_ge(s["qA%d" % i], 1)
            te.matmul_mx(bank(k, i), T.aq[:, _cols(i)], T.asc[:, _cols(i)], T.bq[:, _cols(k)], T.bsc[:, _cols(k)],
                         True, True).then_inc(s["z%d%d" % (i, k)], 1)

    for k, (dst, sems, m) in enumerate(((relay, ("rc", "rs"), m_relay), (part, ("pa", "pa"), m_part),
                                        (far, ("ca", "ca"), m_far))):
        g.wait_ge(s["gQ%d" % k], 1)
        left += _send(g, T, topo, core, dst, own[k] + "q", _cols(0), sems[0], m)
        left += _send(g, T, topo, core, dst, own[k] + "sc", _cols(0), sems[1], m)
    g.wait_ge(s.sent, left)

    te.wait_ge(s.sQ, 1)
    te.wait_ge(s.sx, 2 * _bits(topo.mask(part, core)))
    te.wait_ge(s.sh, 2 * _bits(topo.mask(helper, far) & topo.mask(helper, core)))
    far_helper = plan[far][3]
    tiles = [("gQ3", 1, core),
             ("pa", 2 * _bits(topo.mask(part, core)), part),
             ("ca", 2 * _bits(topo.mask(far, core)), far),
             ("fa", 2 * _bits(topo.mask(far_helper, core) & topo.mask(far_helper, far)), diag)]
    for t, (sem, cnt, maker) in enumerate(tiles):
        te.wait_ge(s[sem], cnt)
        name = "g%d%d" % (T.rank_of(maker), rank)
        for b in range(4):
            ins = te.matmul_mx(T.dp[:, 512 * b:512 * b + NW], T.sq[:, _cols(b)], T.ssc[:, _cols(b)],
                               T[name + "q"][:], T[name + "sc"][:], t == 0, t == 3)
            if t == 3:
                ins.then_inc(s["dF%d" % b], 1)

    for b in range(4):
        src, out = T.dp[:, 512 * b:512 * b + NW], T.ybuf[:, b:512:4]
        if b % 2 == 0:
            v.wait_ge(s["dF%d" % b], 1)
            v.tensor_copy(out, src).then_inc(s.yc, 1)
        else:
            sc.wait_ge(s["dF%d" % b], 1)
            sc.activation(out, src, ActivationFunctionType.Copy).then_inc(s.yc, 1)
    sy.wait_ge(s.yc, 4)
    sy.dma_start(T.y[:, :], T.ybuf[:]).then_inc(s.st, 16)
    sy.wait_ge(s.st, 16)
